import numpy as np
import ml_dtypes

BF16 = ml_dtypes.bfloat16


def bf(x):
    return np.asarray(x, np.float32).astype(BF16)


def f32(x):
    return np.asarray(x, np.float32)


def f64(x):
    return np.asarray(x).astype(np.float64)


def striped(idx):
    return np.tile(idx.reshape(-1, 16).T, (8, 1))


def rows(idx, k):
    return np.tile(idx, (k, 1))


def look(tab, idx):
    return np.take_along_axis(f64(tab), rows(idx, len(tab)), axis=1)


K, S, V, N, M = 256, 4096, 2048, 2048, 256


def setup_inputs():
    return {"tab": f32(np.random.standard_normal((K, S))), "y": f32(np.random.standard_normal((K, V))), "w": bf(np.random.standard_normal((K, M)) / np.sqrt(K)), "b": f32(0.5 * np.random.standard_normal((M, 1))), "offs": striped(np.random.permutation(S)[:N])}


def reference(tab, y, w, b, offs):
    idx = offs[:16].T.reshape(-1)
    t = look(tab, idx)
    x = 1.0 / (1.0 + np.exp(-t)) * f64(y)
    y = f64(w).T @ x
    return np.maximum(y + f64(b), 0.0)

@@ -1,0 +1,72 @@
+import concourse.mybir as mybir
+
+F32, BF16, U16 = mybir.dt.float32, mybir.dt.bfloat16, mybir.dt.uint16
+ACT = mybir.ActivationFunctionType
+ALU = mybir.AluOpType
+
+P = 128
+PIECE = 512
+LANES = 16
+FLOPS = 2 * 256 * 256 * 2048
+
+
+def tile_lookup_gate_sig_relu_kernel(tc, tab, y, w, b, offs, out):
+    nc = tc.nc
+    rows, table_cols = tab.shape
+    n = y.shape[1]
+    m = w.shape[1]
+    row_blocks, out_blocks, pieces = rows // P, m // P, n // PIECE
+    y_blocks = y.rearrange("(k p) n -> p k n", p=P)
+    out_view = out.rearrange("(h p) n -> p h n", p=P)
+
+    with (
+        tc.tile_pool(name="held", bufs=1) as held,
+        tc.psum_pool(name="psum", bufs=1) as psum,
+    ):
+        offsets = held.tile([P, n // LANES], U16, name="offsets")
+        nc.sync.dma_start(offsets[:], offs)
+        windows = [held.tile([P, table_cols], F32, name=f"window{k}") for k in range(row_blocks)]
+        for k in range(row_blocks):
+            nc.sync.dma_start(windows[k][:], tab[k * P:(k + 1) * P, :])
+        weights = held.tile([P, row_blocks, m], BF16, name="weights")
+        nc.sync.dma_start(weights[:], w.rearrange("(k p) m -> p k m", p=P))
+        bias = [held.tile([P, 1], F32, name=f"bias{h}") for h in range(out_blocks)]
+        for h in range(out_blocks):
+            nc.scalar.dma_start(bias[h][:], b[h * P:(h + 1) * P, :])
+        stream = [held.tile([P, row_blocks, PIECE], F32, name=f"stream{j}") for j in range(pieces)]
+        for j in range(pieces):
+            nc.sync.dma_start(stream[j][:], y_blocks[:, :, j * PIECE:(j + 1) * PIECE])
+
+        gates = [[held.tile([P, PIECE], F32, name=f"gate{k}_{j}") for j in range(pieces)] for k in range(row_blocks)]
+        banks = [[psum.tile([P, PIECE], F32, name=f"bank{j}_{h}") for h in range(out_blocks)] for j in range(pieces)]
+
+        def look_up(k, j):
+            piece = offsets[:, j * PIECE // LANES:(j + 1) * PIECE // LANES]
+            nc.scalar.activation(gates[k][j][:], windows[k][:].indirect(piece), ACT.Sigmoid)
+
+        def project(j):
+            for k in range(row_blocks):
+                x = held.tile([P, PIECE], BF16, name=f"x{k}_{j}")
+                nc.vector.tensor_tensor(x[:], gates[k][j][:], stream[j][:, k, :], ALU.mult)
+                for h in range(out_blocks):
+                    nc.tensor.matmul(banks[j][h][:], weights[:, k, h * P:(h + 1) * P], x[:],
+                                     start=(k == 0), stop=(k == row_blocks - 1))
+
+        def finish(j):
+            result = held.tile([P, out_blocks, PIECE], F32, name=f"result{j}")
+            for h in range(out_blocks):
+                if h % 2 == 0:
+                    nc.vector.tensor_scalar(result[:, h, :], banks[j][h][:], bias[h][:], 0.0, ALU.add, ALU.max)
+                else:
+                    nc.scalar.activation(result[:, h, :], banks[j][h][:], ACT.Relu, bias=bias[h][:])
+            nc.sync.dma_start(out_view[:, :, j * PIECE:(j + 1) * PIECE], result[:])
+
+        for k in range(row_blocks - 1):
+            for j in range(pieces):
+                look_up(k, j)
+        for j in range(pieces):
+            look_up(row_blocks - 1, j)
+            project(j)
+            if j > 0:
+                finish(j - 1)
+        finish(pieces - 1)

@@ -16,56 +16,58 @@ def tile_lookup_gate_sig_relu_kernel(tc, tab, y, w, b, offs, out):
     n = y.shape[1]
     m = w.shape[1]
     row_blocks, out_blocks, pieces = rows // P, m // P, n // PIECE
-    y_blocks = y.rearrange("(k p) n -> p k n", p=P)
-    out_view = out.rearrange("(h p) n -> p h n", p=P)
 
     with (
         tc.tile_pool(name="held", bufs=1) as held,
         tc.psum_pool(name="psum", bufs=1) as psum,
     ):
+        warm_in = held.tile([P, 1], F32, name="warm_in")
+        nc.vector.memset(warm_in[:], 0.0)
+        warm_out = held.tile([P, 1], F32, name="warm_out")
+        nc.scalar.activation(warm_out[:], warm_in[:], ACT.Sigmoid)
+
         offsets = held.tile([P, n // LANES], U16, name="offsets")
         nc.sync.dma_start(offsets[:], offs)
         windows = [held.tile([P, table_cols], F32, name=f"window{k}") for k in range(row_blocks)]
-        for k in range(row_blocks):
-            nc.sync.dma_start(windows[k][:], tab[k * P:(k + 1) * P, :])
+        nc.sync.dma_start(windows[0][:], tab[:P, :])
         weights = held.tile([P, row_blocks, m], BF16, name="weights")
         nc.sync.dma_start(weights[:], w.rearrange("(k p) m -> p k m", p=P))
         bias = [held.tile([P, 1], F32, name=f"bias{h}") for h in range(out_blocks)]
         for h in range(out_blocks):
-            nc.scalar.dma_start(bias[h][:], b[h * P:(h + 1) * P, :])
-        stream = [held.tile([P, row_blocks, PIECE], F32, name=f"stream{j}") for j in range(pieces)]
+            nc.sync.dma_start(bias[h][:], b[h * P:(h + 1) * P, :])
+        for k in range(1, row_blocks):
+            nc.sync.dma_start(windows[k][:], tab[k * P:(k + 1) * P, :])
+        stream = [[held.tile([P, PIECE], F32, name=f"stream{j}_{k}") for k in range(row_blocks)] for j in range(pieces)]
         for j in range(pieces):
-            nc.sync.dma_start(stream[j][:], y_blocks[:, :, j * PIECE:(j + 1) * PIECE])
+            for k in range(row_blocks):
+                nc.sync.dma_start(stream[j][k][:], y[k * P:(k + 1) * P, j * PIECE:(j + 1) * PIECE])
 
         gates = [[held.tile([P, PIECE], F32, name=f"gate{k}_{j}") for j in range(pieces)] for k in range(row_blocks)]
         banks = [[psum.tile([P, PIECE], F32, name=f"bank{j}_{h}") for h in range(out_blocks)] for j in range(pieces)]
 
-        def look_up(k, j):
-            piece = offsets[:, j * PIECE // LANES:(j + 1) * PIECE // LANES]
-            nc.scalar.activation(gates[k][j][:], windows[k][:].indirect(piece), ACT.Sigmoid)
+        for k in range(row_blocks):
+            for j in range(pieces):
+                listed = offsets[:, j * PIECE // LANES:(j + 1) * PIECE // LANES]
+                nc.scalar.activation(gates[k][j][:], windows[k][:].indirect(listed), ACT.Sigmoid)
 
         def project(j):
             for k in range(row_blocks):
                 x = held.tile([P, PIECE], BF16, name=f"x{k}_{j}")
-                nc.vector.tensor_tensor(x[:], gates[k][j][:], stream[j][:, k, :], ALU.mult)
+                nc.vector.tensor_tensor(x[:], gates[k][j][:], stream[j][k][:], ALU.mult)
                 for h in range(out_blocks):
                     nc.tensor.matmul(banks[j][h][:], weights[:, k, h * P:(h + 1) * P], x[:],
                                      start=(k == 0), stop=(k == row_blocks - 1))
 
         def finish(j):
-            result = held.tile([P, out_blocks, PIECE], F32, name=f"result{j}")
             for h in range(out_blocks):
-                if h % 2 == 0:
-                    nc.vector.tensor_scalar(result[:, h, :], banks[j][h][:], bias[h][:], 0.0, ALU.add, ALU.max)
+                result = held.tile([P, PIECE], F32, name=f"result{j}_{h}")
+                if j == 0 or (j == pieces - 1 and h % 2 == 0):
+                    nc.vector.tensor_scalar(result[:], banks[j][h][:], bias[h][:], 0.0, ALU.add, ALU.max)
                 else:
-                    nc.scalar.activation(result[:, h, :], banks[j][h][:], ACT.Relu, bias=bias[h][:])
-            nc.sync.dma_start(out_view[:, :, j * PIECE:(j + 1) * PIECE], result[:])
+                    nc.scalar.activation(result[:], banks[j][h][:], ACT.Relu, bias=bias[h][:])
+                nc.sync.dma_start(out[h * P:(h + 1) * P, j * PIECE:(j + 1) * PIECE], result[:])
 
-        for k in range(row_blocks - 1):
-            for j in range(pieces):
-                look_up(k, j)
         for j in range(pieces):
-            look_up(row_blocks - 1, j)
             project(j)
             if j > 0:
                 finish(j - 1)

import concourse.mybir as mybir

F32, BF16, U16 = mybir.dt.float32, mybir.dt.bfloat16, mybir.dt.uint16
ACT = mybir.ActivationFunctionType
ALU = mybir.AluOpType

P = 128
PIECE = 512
LANES = 16
FLOPS = 2 * 256 * 256 * 2048


def tile_lookup_gate_sig_relu_kernel(tc, tab, y, w, b, offs, out):
    nc = tc.nc
    rows, table_cols = tab.shape
    n = y.shape[1]
    m = w.shape[1]
    row_blocks, out_blocks, pieces = rows // P, m // P, n // PIECE

    with (
        tc.tile_pool(name="held", bufs=1) as held,
        tc.psum_pool(name="psum", bufs=1) as psum,
    ):
        warm_in = held.tile([P, 1], F32, name="warm_in")
        nc.vector.memset(warm_in[:], 0.0)
        warm_out = held.tile([P, 1], F32, name="warm_out")
        nc.scalar.activation(warm_out[:], warm_in[:], ACT.Sigmoid)

        offsets = held.tile([P, n // LANES], U16, name="offsets")
        nc.sync.dma_start(offsets[:], offs)
        windows = [held.tile([P, table_cols], F32, name=f"window{k}") for k in range(row_blocks)]
        nc.sync.dma_start(windows[0][:], tab[:P, :])
        weights = held.tile([P, row_blocks, m], BF16, name="weights")
        nc.sync.dma_start(weights[:], w.rearrange("(k p) m -> p k m", p=P))
        bias = [held.tile([P, 1], F32, name=f"bias{h}") for h in range(out_blocks)]
        for h in range(out_blocks):
            nc.sync.dma_start(bias[h][:], b[h * P:(h + 1) * P, :])
        for k in range(1, row_blocks):
            nc.sync.dma_start(windows[k][:], tab[k * P:(k + 1) * P, :])
        stream = [[held.tile([P, PIECE], F32, name=f"stream{j}_{k}") for k in range(row_blocks)] for j in range(pieces)]
        for j in range(pieces):
            for k in range(row_blocks):
                nc.sync.dma_start(stream[j][k][:], y[k * P:(k + 1) * P, j * PIECE:(j + 1) * PIECE])

        gates = [[held.tile([P, PIECE], F32, name=f"gate{k}_{j}") for j in range(pieces)] for k in range(row_blocks)]
        banks = [[psum.tile([P, PIECE], F32, name=f"bank{j}_{h}") for h in range(out_blocks)] for j in range(pieces)]

        for k in range(row_blocks):
            for j in range(pieces):
                listed = offsets[:, j * PIECE // LANES:(j + 1) * PIECE // LANES]
                nc.scalar.activation(gates[k][j][:], windows[k][:].indirect(listed), ACT.Sigmoid)

        def project(j):
            for k in range(row_blocks):
                x = held.tile([P, PIECE], BF16, name=f"x{k}_{j}")
                nc.vector.tensor_tensor(x[:], gates[k][j][:], stream[j][k][:], ALU.mult)
                for h in range(out_blocks):
                    nc.tensor.matmul(banks[j][h][:], weights[:, k, h * P:(h + 1) * P], x[:],
                                     start=(k == 0), stop=(k == row_blocks - 1))

        def finish(j):
            for h in range(out_blocks):
                result = held.tile([P, PIECE], F32, name=f"result{j}_{h}")
                if j == 0 or (j == pieces - 1 and h % 2 == 0):
                    nc.vector.tensor_scalar(result[:], banks[j][h][:], bias[h][:], 0.0, ALU.add, ALU.max)
                else:
                    nc.scalar.activation(result[:], banks[j][h][:], ACT.Relu, bias=bias[h][:])
                nc.sync.dma_start(out[h * P:(h + 1) * P, j * PIECE:(j + 1) * PIECE], result[:])

        for j in range(pieces):
            project(j)
            if j > 0:
                finish(j - 1)
        finish(pieces - 1)
